import numpy as np
import ml_dtypes


def mxq(x, axis, fmt="e4m3"):
    dtype, down = {"e4m3": (ml_dtypes.float8_e4m3fn, 7), "e5m2": (ml_dtypes.float8_e5m2, 14)}[fmt]
    v = np.moveaxis(np.asarray(x, np.float32).astype(ml_dtypes.bfloat16).astype(np.float64), axis, -1)
    blocks = v.reshape(v.shape[:-1] + (-1, 32))
    amax = np.abs(blocks).max(-1, keepdims=True)
    byte = np.maximum(np.where(amax > 0, np.frexp(amax)[1] - 1 + 127, 0) - down, 1)
    scale = np.exp2(byte - 127.0)
    codes = (blocks / scale).astype(np.float32).astype(dtype).astype(np.float64)
    return np.moveaxis((codes * scale).reshape(v.shape), -1, axis)


WIDE = False


def mx_kscale(k):
    if not WIDE:
        return np.ones(k)
    levels = np.array([10, -10, 5, -5, 0])
    if k % 512:
        return np.exp2(np.random.permutation(np.resize(levels, k // 32))).repeat(32)
    a = np.empty((k // 512, 16))
    for p in range(k // 512):
        a[p, :8] = np.random.permutation(np.resize(levels, 8))
        for g in range(8):
            far = levels[np.abs(levels - a[p, g]) >= 10]
            a[p, g + 8] = far[np.random.randint(len(far))]
    return np.exp2(a.ravel()).repeat(32)


def f64(x):
    return np.asarray(x).astype(np.float64)


def striped(idx):
    return np.tile(idx.reshape(-1, 16).T, (8, 1)).astype(np.uint16)


def unstriped(offs):
    return offs[:16].T.reshape(-1).astype(np.int64)


E2M1 = np.array([0.0, 0.5, 1.0, 1.5, 2.0, 3.0, 4.0, 6.0, -0.0, -0.5, -1.0, -1.5, -2.0, -3.0, -4.0, -6.0])


def pack_weight(w, fmt):
    k, n = w.shape
    w = f64(np.asarray(w, np.float32).astype(ml_dtypes.bfloat16)).reshape(k // 32, 32, n)
    amax = np.abs(w).max(1)
    if fmt == "e4m3":
        byte = np.frexp(amax)[1] - 1 + 127 - 7
    else:
        mant, ex = np.frexp(amax / 6.0)
        byte = np.where(mant > 0.5, ex, ex - 1) + 127
    byte = np.clip(np.where(amax > 0, byte, 1), 1, 254)
    scaled = (w * np.exp2(127.0 - byte)[:, None, :]).reshape(k, n).astype(np.float32)
    by_word = np.ascontiguousarray(scaled.reshape(k // 512, 128, 4, n).transpose(0, 1, 3, 2))
    if fmt == "e4m3":
        words = by_word.astype(ml_dtypes.float8_e4m3fn).view(np.uint8)
    else:
        c = by_word.astype(ml_dtypes.float4_e2m1fn).view(np.uint8) & 0xF
        words = (c[..., 0::2] | (c[..., 1::2] << 4)).reshape(k // 512, 128, 2 * n)
    return np.ascontiguousarray(words), np.ascontiguousarray(byte.astype(np.uint8).reshape(k // 512, 16, n))


def unpack_weight(words, scales, fmt):
    g, _, n = scales.shape
    words = np.ascontiguousarray(words).reshape(g, 128, n, -1)
    if fmt == "e4m3":
        vals = words.view(ml_dtypes.float8_e4m3fn).astype(np.float64)
    else:
        nib = np.empty((g, 128, n, 4), np.uint8)
        nib[..., 0::2] = words & 0xF
        nib[..., 1::2] = words >> 4
        vals = E2M1[nib]
    vals = vals * np.repeat(np.exp2(scales.astype(np.float64) - 127.0), 8, axis=1)[..., None]
    return vals.transpose(0, 1, 3, 2).reshape(g * 512, n)


def gelu(v):
    return 0.5 * v * (1.0 + np.tanh(np.sqrt(2.0 / np.pi) * (v + 0.044715 * v**3)))


def pack_table4(v):
    words, scales = pack_weight(v, "e2m1")
    g, t = words.shape[0] // 2, v.shape[1]
    words = words.reshape(g, 2, 128, t, 2).transpose(0, 2, 3, 1, 4)
    return np.concatenate([words.reshape(g, -1), scales.reshape(g, -1)], axis=1)


def unpack_table4(tab):
    g, t = tab.shape[0], tab.shape[1] // 544
    words = tab[:, :512 * t].reshape(g, 128, t, 2, 2).transpose(0, 3, 1, 2, 4).reshape(2 * g, 128, 2 * t)
    return unpack_weight(words, tab[:, 512 * t:].reshape(2 * g, 16, t), "e2m1")


K, T, S, H, N = 1024, 2048, 1024, 1536, 1024

def setup_inputs():
    n = np.random.standard_normal
    s = mx_kscale(K)[:, None]
    u = mx_kscale(H)[:, None]
    w2_words, w2_scales = pack_weight(n((H, N)) / np.sqrt(H) / u, "e2m1")
    return {
        "tab": pack_table4(n((K, T)) * s),
        "offs": striped(np.random.permutation(T)[:S]),
        "w1": (n((K, H)) / np.sqrt(K) / s).astype(np.float32),
        "b1": (0.3 * n(H)).astype(np.float32),
        "gain": (np.random.uniform(0.5, 1.5, H) * u[:, 0]).astype(np.float32),
        "w2_words": w2_words,
        "w2_scales": w2_scales,
        "b2": (0.3 * n(N)).astype(np.float32),
    }

def reference(tab, offs, w1, b1, gain, w2_words, w2_scales, b2):
    v = unpack_table4(tab)[:, unstriped(offs)]
    w1q = mxq(f64(w1), 0, "e4m3")
    a = (w1q.T @ v) + f64(b1)[:, None]
    r = np.maximum(a, 0.0)
    h = np.square(r) * f64(gain)[:, None]
    hq = mxq(h, 0, "e4m3")
    w2 = unpack_weight(w2_words, w2_scales, "e2m1")
    y = w2.T @ hq
    return y + f64(b2)[:, None]

@@ -1,0 +1,227 @@
+from contextlib import ExitStack
+
+import concourse.mybir as mybir
+
+K, T, S, H, N = 1024, 2048, 1024, 1536, 1024
+FLOPS = 2 * K * H * S + 2 * H * N * S
+
+F32 = mybir.dt.float32
+BF16 = mybir.dt.bfloat16
+I32 = mybir.dt.int32
+U32 = mybir.dt.uint32
+U16 = mybir.dt.uint16
+U8 = mybir.dt.uint8
+FP8X4 = mybir.dt.float8_e4m3fn_x4
+FP4X4 = mybir.dt.float4_e2m1fn_x4
+ACT = mybir.ActivationFunctionType
+ALU = mybir.AluOpType
+
+P = 128
+PACK = 4
+K_PASS = P * PACK
+TOK = 512
+UP_PASSES = K // K_PASS
+GROUPS = H // K_PASS
+HALVES = S // TOK
+N_TILES = N // P
+UP_BANKS = 3
+DOWN_BANKS = 5
+SQRT_FLOOR = 2.0**-100
+SCALAR_SQUARE_TOKENS = [384,384,384,384,384,256]
+SCALAR_CASTS = [[128,128],[0,0],[0,0]]
+SCALAR_EVICTS = [[1,1],[1,3],[1,5],[1,7]]
+
+
+def tile_list_paged_squared_relu_kernel(tc, tab, offs, w1, b1, gain, w2_words, w2_scales, b2, out):
+    nc = tc.nc
+    with ExitStack() as ctx:
+        keep = ctx.enter_context(tc.tile_pool(name="keep", bufs=1))
+        ring = ctx.enter_context(tc.tile_pool(name="ring", bufs=3))
+        psum = ctx.enter_context(tc.psum_pool(name="psum", bufs=1))
+
+        offsets = keep.tile([P, S // 16], U16, name="offsets")
+        nc.sync.dma_start(offsets[:], offs)
+
+        tab_scales = keep.tile([P, UP_PASSES, T // 4], I32, name="tab_scales", align_bytes=64)
+        nc.vector.memset(tab_scales[:, 0, :], 0)
+        nc.gpsimd.memset(tab_scales[:, 1, :], 0)
+        gain_sb = keep.tile([P, GROUPS, PACK], F32, name="gain_sb")
+        b1_sb = keep.tile([P, GROUPS, PACK], F32, name="b1_sb")
+        nc.sync.dma_start(gain_sb[:], gain.rearrange("(g p t) -> p g t", p=P, t=PACK))
+        nc.sync.dma_start(b1_sb[:], b1.rearrange("(g p t) -> p g t", p=P, t=PACK))
+        scale_rows = tab[0, 512 * T :].rearrange("(h q r t) -> q r h t", h=UP_PASSES, q=4, r=4).bitcast(I32)
+        for q in range(4):
+            nc.sync.dma_start(tab_scales[32 * q : 32 * q + 4], scale_rows[q])
+        w1_raw = {}
+
+        def load_w1(g, a):
+            raw = keep.tile([P, PACK, K_PASS], F32, name="w1_raw_%d_%d" % (g, a))
+            rows = w1[a * K_PASS : (a + 1) * K_PASS, g * K_PASS : (g + 1) * K_PASS]
+            nc.sync.dma_start(raw[:], rows.rearrange("(p j) c -> p j c", j=PACK))
+            w1_raw[g, a] = raw
+
+        pieces = [(g, a) for g in range(GROUPS) for a in range(UP_PASSES)]
+        for g, a in pieces[:2]:
+            load_w1(g, a)
+        tab_words = keep.tile([P, T], I32, name="tab_words", align_bytes=64)
+        nc.sync.dma_start(tab_words[:], tab[0, : 512 * T].rearrange("(p t) -> p t", p=P).bitcast(I32))
+        for g, a in pieces[2:]:
+            load_w1(g, a)
+
+        sign = keep.tile([P, GROUPS, PACK], BF16, name="sign")
+        guess = keep.tile([P, GROUPS * PACK], F32, name="guess")
+        inv = keep.tile([P, GROUPS * PACK], F32, name="inv")
+        clamped = keep.tile([P, GROUPS * PACK], F32, name="clamped")
+        half_ratio = keep.tile([P, GROUPS * PACK], F32, name="half_ratio")
+        root = keep.tile([P, GROUPS * PACK], F32, name="root")
+        root_b1 = keep.tile([P, GROUPS * PACK], F32, name="root_b1")
+        gain_flat = gain_sb[:].rearrange("p g t -> p (g t)")
+        neg = keep.tile([P, GROUPS * PACK], F32, name="neg")
+        nc.vector.tensor_scalar(neg[:], gain_flat, -1.0, SQRT_FLOOR, ALU.mult, ALU.max)
+        nc.vector.tensor_tensor(clamped[:], neg[:], gain_flat, ALU.max)
+        nc.scalar.activation(guess[:], clamped[:], ACT.Sqrt)
+        nc.scalar.activation(sign[:].rearrange("p g t -> p (g t)"), gain_flat, ACT.Sign)
+        nc.vector.reciprocal(inv[:], guess[:])
+        nc.vector.scalar_tensor_tensor(half_ratio[:], clamped[:], 0.5, inv[:], ALU.mult, ALU.mult)
+        nc.vector.scalar_tensor_tensor(root[:], guess[:], 0.5, half_ratio[:], ALU.mult, ALU.add)
+        nc.vector.tensor_tensor(root_b1[:], root[:], b1_sb[:].rearrange("p g t -> p (g t)"), ALU.mult)
+
+        v_codes, v_planes = {}, {}
+
+        def gather_scales(half):
+            window_offsets = offsets[:, half * (TOK // 16) : (half + 1) * (TOK // 16)]
+            for a in range(UP_PASSES):
+                plane = keep.tile([P, TOK], U8, name="v_plane_%d_%d" % (half, a), align_bytes=64)
+                nc.vector.tensor_copy(plane[:], tab_scales[:, a, :].bitcast(U8).indirect(window_offsets))
+                v_planes[half, a] = plane
+
+        def gather_words(half):
+            window_offsets = offsets[:, half * (TOK // 16) : (half + 1) * (TOK // 16)]
+            pairs = keep.tile([P, TOK], U32, name="v_pairs_%d" % half, align_bytes=64)
+            nc.vector.tensor_copy(pairs[:], tab_words[:].bitcast(U32).indirect(window_offsets))
+            parted = keep.tile([P, UP_PASSES, 2 * TOK], U8, name="v_codes_%d" % half, align_bytes=64)
+            nc.vector.tensor_copy(parted[:].bitcast(U16), pairs[:].bitcast(U16).rearrange("p (j h) -> p h j", h=2))
+            v_codes[half] = parted
+
+        w1_codes, w1_planes = {}, {}
+
+        def quantise_w1(g, passes=range(UP_PASSES)):
+            for a in passes:
+                raw = w1_raw[g, a]
+                grouped = keep.tile([P, PACK * K_PASS], BF16, name="w1_grouped", tag="stage_%d_%d" % (g, a), align_bytes=64)
+                dst = grouped[:].rearrange("p (t m j) -> p m t j", t=PACK, j=PACK)
+                src = raw[:].rearrange("p j (m t) -> p m t j", t=PACK)
+                split = SCALAR_CASTS[g][a]
+                if split > 0:
+                    nc.scalar.copy(dst[:, :split], src[:, :split])
+                if split < P:
+                    nc.vector.tensor_copy(dst[:, split:], src[:, split:])
+                codes = keep.tile([P, K_PASS], U32, name="w1_codes_%d_%d" % (g, a), align_bytes=64)
+                plane = keep.tile([P, K_PASS], U8, name="w1_plane_%d_%d" % (g, a), align_bytes=64)
+                nc.vector.quantize_mx(codes[:].bitcast(FP8X4), plane[:], grouped[:])
+                w1_codes[g, a], w1_planes[g, a] = codes, plane
+
+        def load_w2():
+            planes = keep.tile([P, GROUPS, N // 4], I32, name="w2_planes", tag="stage_1_0", align_bytes=64)
+            nc.vector.memset(planes[:], 0)
+            rows = w2_scales.rearrange("a (q r) n -> q r a n", r=4).bitcast(I32)
+            for q in range(4):
+                nc.sync.dma_start(planes[32 * q : 32 * q + 4], rows[q])
+            codes = keep.tile([P, GROUPS, N // 2], I32, name="w2_codes", tag="stage_1_1", align_bytes=64)
+            nc.sync.dma_start(codes[:], w2_words.rearrange("a p n -> p a n").bitcast(I32))
+            bias = keep.tile([P, N_TILES], F32, name="b2_sb", tag="stage_2_0", align_bytes=64)
+            with nc.allow_non_contiguous_dma("one bias value for each partition"):
+                nc.sync.dma_start(bias[:], b2.rearrange("(j p) -> p j", p=P))
+            return codes, planes, bias
+
+        banks = [psum.tile([P, TOK], F32, name="bank_%d" % b) for b in range(UP_BANKS + DOWN_BANKS)]
+        h_codes, h_planes = {}, {}
+
+        def hidden(g, half):
+            unit = len(h_codes)
+            relu = ring.tile([P, PACK, TOK], F32, name="relu")
+            for t in range(PACK):
+                bank = banks[(unit * PACK + t) % UP_BANKS]
+                cols = slice(t * P, (t + 1) * P)
+                for a in range(UP_PASSES):
+                    nc.tensor.matmul_mx(
+                        out=bank[:],
+                        lhsT=w1_codes[g, a][:, cols].bitcast(FP8X4),
+                        lhsT_scale=w1_planes[g, a][:, cols],
+                        rhs=v_codes[half][:, a, :].bitcast(FP4X4),
+                        rhs_scale=v_planes[half, a][:],
+                        start=(a == 0),
+                        stop=(a == UP_PASSES - 1),
+                    )
+                c = g * PACK + t
+                nc.scalar.activation(relu[:, t, :], bank[:], ACT.Relu, bias=root_b1[:, c : c + 1], scale=root[:, c : c + 1])
+            squared = ring.tile([P, TOK, PACK], BF16, name="squared", align_bytes=64)
+            split = SCALAR_SQUARE_TOKENS[unit]
+            src = relu[:].rearrange("p t (c i) -> p c t i", i=4)
+            dst = squared[:].rearrange("p (c i) t -> p c t i", i=4)
+            if split > 0:
+                nc.scalar.activation(dst[:, : split // 4], src[:, : split // 4], ACT.Square)
+            if split < TOK:
+                nc.vector.tensor_tensor(dst[:, split // 4 :], src[:, split // 4 :], src[:, split // 4 :], ALU.mult)
+            signed = ring.tile([P, TOK, PACK], BF16, name="signed", align_bytes=64)
+            nc.vector.tensor_tensor(signed[:], squared[:], sign[:, g : g + 1, :].to_broadcast([P, TOK, PACK]), ALU.mult)
+            codes = keep.tile([P, TOK], U32, name="h_codes_%d" % unit, align_bytes=64)
+            plane = keep.tile([P, TOK], U8, name="h_plane_%d" % unit, align_bytes=64)
+            nc.vector.quantize_mx(codes[:].bitcast(FP8X4), plane[:], signed[:].rearrange("p s t -> p (s t)"))
+            h_codes[g, half], h_planes[g, half] = codes, plane
+
+        def down_bank(half, n):
+            if half == HALVES - 1 and n >= DOWN_BANKS:
+                return banks[n - DOWN_BANKS]
+            return banks[UP_BANKS + (half * N_TILES + n) % DOWN_BANKS]
+
+        def down_pass(g, half, n):
+            nc.tensor.matmul_mx(
+                out=down_bank(half, n)[:],
+                lhsT=w2_codes[:, g, :].bitcast(U8)[:, 2 * n * P : 2 * (n + 1) * P].bitcast(FP4X4),
+                lhsT_scale=w2_planes[:, g, :].bitcast(U8)[:, n * P : (n + 1) * P],
+                rhs=h_codes[g, half][:].bitcast(FP8X4),
+                rhs_scale=h_planes[g, half][:],
+                start=(g == 0),
+                stop=(g == GROUPS - 1),
+            )
+
+        def finish(half, n):
+            result = keep.tile([P, TOK], F32, name="result_%d_%d" % (half, n))
+            if [half, n] in SCALAR_EVICTS:
+                nc.scalar.activation(result[:], down_bank(half, n)[:], ACT.Identity, bias=b2_sb[:, n : n + 1])
+            else:
+                nc.vector.tensor_scalar(result[:], down_bank(half, n)[:], b2_sb[:, n : n + 1], None, ALU.add)
+            nc.sync.dma_start(out[n * P : (n + 1) * P, half * TOK : (half + 1) * TOK], result[:])
+
+        early = range(DOWN_BANKS)
+        late = range(DOWN_BANKS, N_TILES)
+        gather_scales(0)
+        quantise_w1(0)
+        gather_words(0)
+        gather_scales(1)
+        hidden(0, 0)
+        quantise_w1(1)
+        hidden(1, 0)
+        quantise_w1(2)
+        w2_codes, w2_planes, b2_sb = load_w2()
+        hidden(2, 0)
+        gather_words(1)
+        hidden(0, 1)
+        for g in range(GROUPS):
+            for n in early:
+                down_pass(g, 0, n)
+        for n in early:
+            finish(0, n)
+        hidden(1, 1)
+        for n in late:
+            for g in range(GROUPS):
+                down_pass(g, 0, n)
+            finish(0, n)
+        hidden(2, 1)
+        for g in range(GROUPS - 1):
+            for n in range(N_TILES):
+                down_pass(g, 1, n)
+        for n in range(N_TILES):
+            down_pass(GROUPS - 1, 1, n)
+            finish(1, n)

@@ -24,12 +24,15 @@ UP_PASSES = K // K_PASS
 GROUPS = H // K_PASS
 HALVES = S // TOK
 N_TILES = N // P
-UP_BANKS = 3
-DOWN_BANKS = 5
 SQRT_FLOOR = 2.0**-100
-SCALAR_SQUARE_TOKENS = [384,384,384,384,384,256]
-SCALAR_CASTS = [[128,128],[0,0],[0,0]]
-SCALAR_EVICTS = [[1,1],[1,3],[1,5],[1,7]]
+UP_BANKS = 4
+DOWN_BANKS = 4
+PRE = 1
+SCALAR_CASTS = [[48, 64], [64, 0], [48, 32]]
+SCALAR_EVICTS = [[0, 0], [0, 4], [1, 1], [1, 3], [1, 4], [1, 7]]
+FIRST = (0, 0)
+LOADS = [["words", (0, 1)], ["words", (0, 1)], [(0, 1), "words"]][PRE] + [(1, 0), (1, 1), (2, 0), (2, 1)]
+SLOT = {(0, 0): "first", LOADS[0]: "neg", LOADS[1]: "gain_sb", (1, 0): "clamped", (1, 1): "inv", (2, 0): "guess", (2, 1): "half_ratio"}
 
 
 def tile_list_paged_squared_relu_kernel(tc, tab, offs, w1, b1, gain, w2_words, w2_scales, b2, out):
@@ -43,10 +46,11 @@ def tile_list_paged_squared_relu_kernel(tc, tab, offs, w1, b1, gain, w2_words, w
         nc.sync.dma_start(offsets[:], offs)
 
         tab_scales = keep.tile([P, UP_PASSES, T // 4], I32, name="tab_scales", align_bytes=64)
-        nc.vector.memset(tab_scales[:, 0, :], 0)
-        nc.gpsimd.memset(tab_scales[:, 1, :], 0)
+        flat_scales = tab_scales[:].rearrange("p h t -> p (h t)")
+        nc.vector.memset(flat_scales[:, :768], 0)
+        nc.gpsimd.memset(flat_scales[:, 768:], 0)
         gain_sb = keep.tile([P, GROUPS, PACK], F32, name="gain_sb")
-        b1_sb = keep.tile([P, GROUPS, PACK], F32, name="b1_sb")
+        b1_sb = keep.tile([P, GROUPS, PACK], F32, name="b1_sb", align_bytes=64)
         nc.sync.dma_start(gain_sb[:], gain.rearrange("(g p t) -> p g t", p=P, t=PACK))
         nc.sync.dma_start(b1_sb[:], b1.rearrange("(g p t) -> p g t", p=P, t=PACK))
         scale_rows = tab[0, 512 * T :].rearrange("(h q r t) -> q r h t", h=UP_PASSES, q=4, r=4).bitcast(I32)
@@ -55,18 +59,25 @@ def tile_list_paged_squared_relu_kernel(tc, tab, offs, w1, b1, gain, w2_words, w
         w1_raw = {}
 
         def load_w1(g, a):
-            raw = keep.tile([P, PACK, K_PASS], F32, name="w1_raw_%d_%d" % (g, a))
+            raw = keep.tile([P, PACK, K_PASS], F32, name="w1_raw_%d_%d" % (g, a), tag=SLOT[g, a])
             rows = w1[a * K_PASS : (a + 1) * K_PASS, g * K_PASS : (g + 1) * K_PASS]
             nc.sync.dma_start(raw[:], rows.rearrange("(p j) c -> p j c", j=PACK))
             w1_raw[g, a] = raw
 
-        pieces = [(g, a) for g in range(GROUPS) for a in range(UP_PASSES)]
-        for g, a in pieces[:2]:
-            load_w1(g, a)
-        tab_words = keep.tile([P, T], I32, name="tab_words", align_bytes=64)
-        nc.sync.dma_start(tab_words[:], tab[0, : 512 * T].rearrange("(p t) -> p t", p=P).bitcast(I32))
-        for g, a in pieces[2:]:
-            load_w1(g, a)
+        load_w1(*FIRST)
+
+        def load_w2():
+            planes = keep.tile([P, GROUPS, N // 4], I32, name="w2_planes", tag="w1_grouped_0_0", align_bytes=64)
+            nc.vector.memset(planes[:], 0)
+            rows = w2_scales.rearrange("a (q r) n -> q r a n", r=4).bitcast(I32)
+            for q in range(4):
+                nc.sync.dma_start(planes[32 * q : 32 * q + 4], rows[q])
+            codes = keep.tile([P, GROUPS, N // 2], I32, name="w2_codes", tag="b1_sb", align_bytes=64)
+            nc.sync.dma_start(codes[:], w2_words.rearrange("a p n -> p a n").bitcast(I32))
+            bias = keep.tile([P, N_TILES], F32, name="b2_sb", tag="w1_grouped_0_1", align_bytes=64)
+            with nc.allow_non_contiguous_dma("one bias value for each partition"):
+                nc.sync.dma_start(bias[:], b2.rearrange("(j p) -> p j", p=P))
+            return codes, planes, bias
 
         sign = keep.tile([P, GROUPS, PACK], BF16, name="sign")
         guess = keep.tile([P, GROUPS * PACK], F32, name="guess")
@@ -85,6 +96,13 @@ def tile_list_paged_squared_relu_kernel(tc, tab, offs, w1, b1, gain, w2_words, w
         nc.vector.scalar_tensor_tensor(half_ratio[:], clamped[:], 0.5, inv[:], ALU.mult, ALU.mult)
         nc.vector.scalar_tensor_tensor(root[:], guess[:], 0.5, half_ratio[:], ALU.mult, ALU.add)
         nc.vector.tensor_tensor(root_b1[:], root[:], b1_sb[:].rearrange("p g t -> p (g t)"), ALU.mult)
+
+        tab_words = keep.tile([P, T], I32, name="tab_words", tag=SLOT["words"])
+        for piece in LOADS:
+            if piece == "words":
+                nc.sync.dma_start(tab_words[:], tab[0, : 512 * T].rearrange("(p t) -> p t", p=P).bitcast(I32))
+            else:
+                load_w1(*piece)
 
         v_codes, v_planes = {}, {}
 
@@ -108,9 +126,9 @@ def tile_list_paged_squared_relu_kernel(tc, tab, offs, w1, b1, gain, w2_words, w
         def quantise_w1(g, passes=range(UP_PASSES)):
             for a in passes:
                 raw = w1_raw[g, a]
-                grouped = keep.tile([P, PACK * K_PASS], BF16, name="w1_grouped", tag="stage_%d_%d" % (g, a), align_bytes=64)
-                dst = grouped[:].rearrange("p (t m j) -> p m t j", t=PACK, j=PACK)
-                src = raw[:].rearrange("p j (m t) -> p m t j", t=PACK)
+                grouped = keep.tile([P, PACK * K_PASS], BF16, name="w1_grouped_%d_%d" % (g, a), align_bytes=64)
+                dst = grouped[:].rearrange("p (t m j) -> p m j t", t=PACK, j=PACK)
+                src = raw[:].rearrange("p j (m t) -> p m j t", t=PACK)
                 split = SCALAR_CASTS[g][a]
                 if split > 0:
                     nc.scalar.copy(dst[:, :split], src[:, :split])
@@ -121,52 +139,45 @@ def tile_list_paged_squared_relu_kernel(tc, tab, offs, w1, b1, gain, w2_words, w
                 nc.vector.quantize_mx(codes[:].bitcast(FP8X4), plane[:], grouped[:])
                 w1_codes[g, a], w1_planes[g, a] = codes, plane
 
-        def load_w2():
-            planes = keep.tile([P, GROUPS, N // 4], I32, name="w2_planes", tag="stage_1_0", align_bytes=64)
-            nc.vector.memset(planes[:], 0)
-            rows = w2_scales.rearrange("a (q r) n -> q r a n", r=4).bitcast(I32)
-            for q in range(4):
-                nc.sync.dma_start(planes[32 * q : 32 * q + 4], rows[q])
-            codes = keep.tile([P, GROUPS, N // 2], I32, name="w2_codes", tag="stage_1_1", align_bytes=64)
-            nc.sync.dma_start(codes[:], w2_words.rearrange("a p n -> p a n").bitcast(I32))
-            bias = keep.tile([P, N_TILES], F32, name="b2_sb", tag="stage_2_0", align_bytes=64)
-            with nc.allow_non_contiguous_dma("one bias value for each partition"):
-                nc.sync.dma_start(bias[:], b2.rearrange("(j p) -> p j", p=P))
-            return codes, planes, bias
-
         banks = [psum.tile([P, TOK], F32, name="bank_%d" % b) for b in range(UP_BANKS + DOWN_BANKS)]
         h_codes, h_planes = {}, {}
 
-        def hidden(g, half):
-            unit = len(h_codes)
-            relu = ring.tile([P, PACK, TOK], F32, name="relu")
-            for t in range(PACK):
-                bank = banks[(unit * PACK + t) % UP_BANKS]
-                cols = slice(t * P, (t + 1) * P)
-                for a in range(UP_PASSES):
-                    nc.tensor.matmul_mx(
-                        out=bank[:],
-                        lhsT=w1_codes[g, a][:, cols].bitcast(FP8X4),
-                        lhsT_scale=w1_planes[g, a][:, cols],
-                        rhs=v_codes[half][:, a, :].bitcast(FP4X4),
-                        rhs_scale=v_planes[half, a][:],
-                        start=(a == 0),
-                        stop=(a == UP_PASSES - 1),
-                    )
-                c = g * PACK + t
-                nc.scalar.activation(relu[:, t, :], bank[:], ACT.Relu, bias=root_b1[:, c : c + 1], scale=root[:, c : c + 1])
-            squared = ring.tile([P, TOK, PACK], BF16, name="squared", align_bytes=64)
-            split = SCALAR_SQUARE_TOKENS[unit]
-            src = relu[:].rearrange("p t (c i) -> p c t i", i=4)
-            dst = squared[:].rearrange("p (c i) t -> p c t i", i=4)
-            if split > 0:
-                nc.scalar.activation(dst[:, : split // 4], src[:, : split // 4], ACT.Square)
-            if split < TOK:
-                nc.vector.tensor_tensor(dst[:, split // 4 :], src[:, split // 4 :], src[:, split // 4 :], ALU.mult)
+        relus, squares = {}, {}
+
+        def up(g, half, t):
+            if t == 0:
+                relus[g, half] = ring.tile([P, PACK, TOK], F32, name="relu")
+            unit = len(relus) - 1
+            bank = banks[(unit * PACK + t) % UP_BANKS]
+            cols = slice(t * P, (t + 1) * P)
+            for a in range(UP_PASSES):
+                nc.tensor.matmul_mx(
+                    out=bank[:],
+                    lhsT=w1_codes[g, a][:, cols].bitcast(FP8X4),
+                    lhsT_scale=w1_planes[g, a][:, cols],
+                    rhs=v_codes[half][:, a, :].bitcast(FP4X4),
+                    rhs_scale=v_planes[half, a][:],
+                    start=(a == 0),
+                    stop=(a == UP_PASSES - 1),
+                )
+            c = g * PACK + t
+            nc.scalar.activation(relus[g, half][:, t, :], bank[:], ACT.Relu, bias=root_b1[:, c : c + 1], scale=root[:, c : c + 1])
+
+        def square(g, half, first, last, on_scalar):
+            if (g, half) not in squares:
+                squares[g, half] = ring.tile([P, TOK, PACK], BF16, name="squared", align_bytes=64)
+            src = relus[g, half][:].rearrange("p t (c i) -> p c t i", i=4)[:, first // 4 : last // 4]
+            dst = squares[g, half][:].rearrange("p (c i) t -> p c t i", i=4)[:, first // 4 : last // 4]
+            if on_scalar:
+                nc.scalar.activation(dst, src, ACT.Square)
+            else:
+                nc.vector.tensor_tensor(dst, src, src, ALU.mult)
+
+        def quantise_h(g, half):
             signed = ring.tile([P, TOK, PACK], BF16, name="signed", align_bytes=64)
-            nc.vector.tensor_tensor(signed[:], squared[:], sign[:, g : g + 1, :].to_broadcast([P, TOK, PACK]), ALU.mult)
-            codes = keep.tile([P, TOK], U32, name="h_codes_%d" % unit, align_bytes=64)
-            plane = keep.tile([P, TOK], U8, name="h_plane_%d" % unit, align_bytes=64)
+            nc.vector.tensor_tensor(signed[:], squares[g, half][:], sign[:, g : g + 1, :].to_broadcast([P, TOK, PACK]), ALU.mult)
+            codes = keep.tile([P, TOK], U32, name="h_codes_%d_%d" % (g, half), align_bytes=64)
+            plane = keep.tile([P, TOK], U8, name="h_plane_%d_%d" % (g, half), align_bytes=64)
             nc.vector.quantize_mx(codes[:].bitcast(FP8X4), plane[:], signed[:].rearrange("p s t -> p (s t)"))
             h_codes[g, half], h_planes[g, half] = codes, plane
 
@@ -197,31 +208,75 @@ def tile_list_paged_squared_relu_kernel(tc, tab, offs, w1, b1, gain, w2_words, w
         early = range(DOWN_BANKS)
         late = range(DOWN_BANKS, N_TILES)
         gather_scales(0)
-        quantise_w1(0)
         gather_words(0)
-        gather_scales(1)
-        hidden(0, 0)
-        quantise_w1(1)
-        hidden(1, 0)
-        quantise_w1(2)
+        quantise_w1(0)
         w2_codes, w2_planes, b2_sb = load_w2()
-        hidden(2, 0)
+        gather_scales(1)
+        quantise_w1(1)
+        up(0, 0, 0)
+        up(0, 0, 1)
+        up(0, 0, 2)
+        up(0, 0, 3)
         gather_words(1)
-        hidden(0, 1)
-        for g in range(GROUPS):
+        quantise_w1(2)
+        square(0, 0, 416, 512, False)
+        up(1, 0, 0)
+        square(0, 0, 0, 208, True)
+        up(1, 0, 1)
+        up(1, 0, 2)
+        square(0, 0, 208, 416, True)
+        up(1, 0, 3)
+        quantise_h(0, 0)
+        square(1, 0, 160, 512, False)
+        up(2, 0, 0)
+        square(1, 0, 0, 80, True)
+        up(2, 0, 1)
+        up(2, 0, 2)
+        square(1, 0, 80, 160, True)
+        up(2, 0, 3)
+        quantise_h(1, 0)
+        square(2, 0, 0, 224, True)
+        square(2, 0, 224, 512, False)
+        quantise_h(2, 0)
+        up(0, 1, 0)
+        up(0, 1, 1)
+        up(0, 1, 2)
+        up(0, 1, 3)
+        for g in range(2):
             for n in early:
                 down_pass(g, 0, n)
         for n in early:
+            down_pass(2, 0, n)
             finish(0, n)
-        hidden(1, 1)
+        square(0, 1, 160, 512, False)
+        up(1, 1, 0)
+        square(0, 1, 0, 80, True)
+        up(1, 1, 1)
+        up(1, 1, 2)
+        square(0, 1, 80, 160, True)
+        up(1, 1, 3)
+        quantise_h(0, 1)
+        square(1, 1, 256, 512, False)
+        up(2, 1, 0)
+        square(1, 1, 0, 128, True)
+        up(2, 1, 1)
+        up(2, 1, 2)
+        square(1, 1, 128, 256, True)
+        up(2, 1, 3)
+        quantise_h(1, 1)
+        square(2, 1, 0, 448, True)
+        square(2, 1, 448, 512, False)
+        quantise_h(2, 1)
         for n in late:
             for g in range(GROUPS):
                 down_pass(g, 0, n)
             finish(0, n)
-        hidden(2, 1)
-        for g in range(GROUPS - 1):
-            for n in range(N_TILES):
-                down_pass(g, 1, n)
+        for n in early:
+            down_pass(0, 1, n)
+        for n in late:
+            down_pass(0, 1, n)
         for n in range(N_TILES):
-            down_pass(GROUPS - 1, 1, n)
+            down_pass(1, 1, n)
+        for n in range(N_TILES):
+            down_pass(2, 1, n)
             finish(1, n)

@@ -27,12 +27,10 @@ N_TILES = N // P
 SQRT_FLOOR = 2.0**-100
 UP_BANKS = 4
 DOWN_BANKS = 4
-PRE = 1
-SCALAR_CASTS = [[48, 64], [64, 0], [48, 32]]
-SCALAR_EVICTS = [[0, 0], [0, 4], [1, 1], [1, 3], [1, 4], [1, 7]]
-FIRST = (0, 0)
-LOADS = [["words", (0, 1)], ["words", (0, 1)], [(0, 1), "words"]][PRE] + [(1, 0), (1, 1), (2, 0), (2, 1)]
-SLOT = {(0, 0): "first", LOADS[0]: "neg", LOADS[1]: "gain_sb", (1, 0): "clamped", (1, 1): "inv", (2, 0): "guess", (2, 1): "half_ratio"}
+PRE = 0
+SCALAR_CASTS = [[128, 96], [96, 0], [0, 0]]
+SCALAR_EVICTS = [[0, 4], [0, 6], [0, 7], [1, 1], [1, 3], [1, 5], [1, 7]]
+SLOT = {(1, 1): 'w1_raw_0_0', 1: 'w1_raw_0_1'}
 
 
 def tile_list_paged_squared_relu_kernel(tc, tab, offs, w1, b1, gain, w2_words, w2_scales, b2, out):
@@ -42,6 +40,10 @@ def tile_list_paged_squared_relu_kernel(tc, tab, offs, w1, b1, gain, w2_words, w
         ring = ctx.enter_context(tc.tile_pool(name="ring", bufs=3))
         psum = ctx.enter_context(tc.psum_pool(name="psum", bufs=1))
 
+        gain_sb = keep.tile([P, GROUPS, PACK], F32, name="gain_sb")
+        b1_sb = keep.tile([P, GROUPS, PACK], F32, name="b1_sb")
+        nc.sync.dma_start(gain_sb[:], gain.rearrange("(g p t) -> p g t", p=P, t=PACK))
+        nc.scalar.dma_start(b1_sb[:], b1.rearrange("(g p t) -> p g t", p=P, t=PACK))
         offsets = keep.tile([P, S // 16], U16, name="offsets")
         nc.sync.dma_start(offsets[:], offs)
 
@@ -49,73 +51,75 @@ def tile_list_paged_squared_relu_kernel(tc, tab, offs, w1, b1, gain, w2_words, w
         flat_scales = tab_scales[:].rearrange("p h t -> p (h t)")
         nc.vector.memset(flat_scales[:, :768], 0)
         nc.gpsimd.memset(flat_scales[:, 768:], 0)
-        gain_sb = keep.tile([P, GROUPS, PACK], F32, name="gain_sb")
-        b1_sb = keep.tile([P, GROUPS, PACK], F32, name="b1_sb", align_bytes=64)
-        nc.sync.dma_start(gain_sb[:], gain.rearrange("(g p t) -> p g t", p=P, t=PACK))
-        nc.sync.dma_start(b1_sb[:], b1.rearrange("(g p t) -> p g t", p=P, t=PACK))
+        width = GROUPS * PACK
+        gain_flat = gain_sb[:].rearrange("p g t -> p (g t)")
+        sign = keep.tile([P, GROUPS, PACK], BF16, name="sign")
+        flipped = keep.tile([P, width], F32, name="flipped")
+        negative = keep.tile([P, width], F32, name="negative")
+        clamped = keep.tile([P, width], F32, name="clamped")
+        guess = keep.tile([P, width], F32, name="guess")
+        inverse = keep.tile([P, width], F32, name="inverse")
+        half_ratio = keep.tile([P, width], F32, name="half_ratio")
+        root = keep.tile([P, width], F32, name="root")
+        root_b1 = keep.tile([P, width], F32, name="root_b1")
+        nc.vector.tensor_scalar(flipped[:], gain_flat, -1.0, SQRT_FLOOR, ALU.mult, ALU.max)
+        nc.vector.tensor_scalar(negative[:], gain_flat, 0.0, None, ALU.is_lt)
+        nc.vector.tensor_tensor(clamped[:], flipped[:], gain_flat, ALU.max)
+        nc.vector.scalar_tensor_tensor(sign[:].rearrange("p g t -> p (g t)"), gain_flat, 0.0, negative[:], ALU.is_gt, ALU.subtract)
+        nc.scalar.activation(guess[:], clamped[:], ACT.Sqrt)
+        nc.vector.reciprocal(inverse[:], guess[:])
+        nc.vector.scalar_tensor_tensor(half_ratio[:], clamped[:], 0.5, inverse[:], ALU.mult, ALU.mult)
+        nc.vector.scalar_tensor_tensor(root[:], guess[:], 0.5, half_ratio[:], ALU.mult, ALU.add)
+        nc.vector.tensor_tensor(root_b1[:], root[:], b1_sb[:].rearrange("p g t -> p (g t)"), ALU.mult)
+
         scale_rows = tab[0, 512 * T :].rearrange("(h q r t) -> q r h t", h=UP_PASSES, q=4, r=4).bitcast(I32)
         for q in range(4):
             nc.sync.dma_start(tab_scales[32 * q : 32 * q + 4], scale_rows[q])
         w1_raw = {}
 
         def load_w1(g, a):
-            raw = keep.tile([P, PACK, K_PASS], F32, name="w1_raw_%d_%d" % (g, a), tag=SLOT[g, a])
+            raw = keep.tile([P, PACK, K_PASS], F32, name="w1_raw_%d_%d" % (g, a), align_bytes=64)
             rows = w1[a * K_PASS : (a + 1) * K_PASS, g * K_PASS : (g + 1) * K_PASS]
             nc.sync.dma_start(raw[:], rows.rearrange("(p j) c -> p j c", j=PACK))
             w1_raw[g, a] = raw
 
-        load_w1(*FIRST)
-
         def load_w2():
-            planes = keep.tile([P, GROUPS, N // 4], I32, name="w2_planes", tag="w1_grouped_0_0", align_bytes=64)
-            nc.vector.memset(planes[:], 0)
+            planes = keep.tile([P, GROUPS, N // 4], I32, name="w2_planes", align_bytes=64)
+            nc.gpsimd.memset(planes[:], 0)
             rows = w2_scales.rearrange("a (q r) n -> q r a n", r=4).bitcast(I32)
             for q in range(4):
                 nc.sync.dma_start(planes[32 * q : 32 * q + 4], rows[q])
-            codes = keep.tile([P, GROUPS, N // 2], I32, name="w2_codes", tag="b1_sb", align_bytes=64)
+            codes = keep.tile([P, GROUPS, N // 2], I32, name="w2_codes", align_bytes=64)
             nc.sync.dma_start(codes[:], w2_words.rearrange("a p n -> p a n").bitcast(I32))
-            bias = keep.tile([P, N_TILES], F32, name="b2_sb", tag="w1_grouped_0_1", align_bytes=64)
+            bias = keep.tile([P, N_TILES], F32, name="b2_sb", align_bytes=64)
             with nc.allow_non_contiguous_dma("one bias value for each partition"):
                 nc.sync.dma_start(bias[:], b2.rearrange("(j p) -> p j", p=P))
             return codes, planes, bias
 
-        sign = keep.tile([P, GROUPS, PACK], BF16, name="sign")
-        guess = keep.tile([P, GROUPS * PACK], F32, name="guess")
-        inv = keep.tile([P, GROUPS * PACK], F32, name="inv")
-        clamped = keep.tile([P, GROUPS * PACK], F32, name="clamped")
-        half_ratio = keep.tile([P, GROUPS * PACK], F32, name="half_ratio")
-        root = keep.tile([P, GROUPS * PACK], F32, name="root")
-        root_b1 = keep.tile([P, GROUPS * PACK], F32, name="root_b1")
-        gain_flat = gain_sb[:].rearrange("p g t -> p (g t)")
-        neg = keep.tile([P, GROUPS * PACK], F32, name="neg")
-        nc.vector.tensor_scalar(neg[:], gain_flat, -1.0, SQRT_FLOOR, ALU.mult, ALU.max)
-        nc.vector.tensor_tensor(clamped[:], neg[:], gain_flat, ALU.max)
-        nc.scalar.activation(guess[:], clamped[:], ACT.Sqrt)
-        nc.scalar.activation(sign[:].rearrange("p g t -> p (g t)"), gain_flat, ACT.Sign)
-        nc.vector.reciprocal(inv[:], guess[:])
-        nc.vector.scalar_tensor_tensor(half_ratio[:], clamped[:], 0.5, inv[:], ALU.mult, ALU.mult)
-        nc.vector.scalar_tensor_tensor(root[:], guess[:], 0.5, half_ratio[:], ALU.mult, ALU.add)
-        nc.vector.tensor_tensor(root_b1[:], root[:], b1_sb[:].rearrange("p g t -> p (g t)"), ALU.mult)
+        pieces = [(g, a) for g in range(GROUPS) for a in range(UP_PASSES)]
+        for g, a in pieces[:PRE]:
+            load_w1(g, a)
+        tab_words = keep.tile([P, T], I32, name="tab_words", align_bytes=64)
+        nc.sync.dma_start(tab_words[:], tab[0, : 512 * T].rearrange("(p t) -> p t", p=P).bitcast(I32))
+        for g, a in pieces[PRE:6]:
+            load_w1(g, a)
 
-        tab_words = keep.tile([P, T], I32, name="tab_words", tag=SLOT["words"])
-        for piece in LOADS:
-            if piece == "words":
-                nc.sync.dma_start(tab_words[:], tab[0, : 512 * T].rearrange("(p t) -> p t", p=P).bitcast(I32))
-            else:
-                load_w1(*piece)
+        w2_codes, w2_planes, b2_sb = load_w2()
+        for g, a in pieces[6:]:
+            load_w1(g, a)
 
         v_codes, v_planes = {}, {}
 
         def gather_scales(half):
             window_offsets = offsets[:, half * (TOK // 16) : (half + 1) * (TOK // 16)]
             for a in range(UP_PASSES):
-                plane = keep.tile([P, TOK], U8, name="v_plane_%d_%d" % (half, a), align_bytes=64)
+                plane = keep.tile([P, TOK], U8, name="v_plane_%d_%d" % (half, a), tag=SLOT.get((half, a), "v_plane_%d_%d" % (half, a)), align_bytes=64)
                 nc.vector.tensor_copy(plane[:], tab_scales[:, a, :].bitcast(U8).indirect(window_offsets))
                 v_planes[half, a] = plane
 
         def gather_words(half):
             window_offsets = offsets[:, half * (TOK // 16) : (half + 1) * (TOK // 16)]
-            pairs = keep.tile([P, TOK], U32, name="v_pairs_%d" % half, align_bytes=64)
+            pairs = keep.tile([P, TOK], U32, name="v_pairs_%d" % half, tag=SLOT.get(half, "v_pairs_%d" % half), align_bytes=64)
             nc.vector.tensor_copy(pairs[:], tab_words[:].bitcast(U32).indirect(window_offsets))
             parted = keep.tile([P, UP_PASSES, 2 * TOK], U8, name="v_codes_%d" % half, align_bytes=64)
             nc.vector.tensor_copy(parted[:].bitcast(U16), pairs[:].bitcast(U16).rearrange("p (j h) -> p h j", h=2))
@@ -173,12 +177,14 @@ def tile_list_paged_squared_relu_kernel(tc, tab, offs, w1, b1, gain, w2_words, w
             else:
                 nc.vector.tensor_tensor(dst, src, src, ALU.mult)
 
-        def quantise_h(g, half):
+        def quantise_h(g, half, pieces=((0, TOK),)):
             signed = ring.tile([P, TOK, PACK], BF16, name="signed", align_bytes=64)
-            nc.vector.tensor_tensor(signed[:], squares[g, half][:], sign[:, g : g + 1, :].to_broadcast([P, TOK, PACK]), ALU.mult)
             codes = keep.tile([P, TOK], U32, name="h_codes_%d_%d" % (g, half), align_bytes=64)
             plane = keep.tile([P, TOK], U8, name="h_plane_%d_%d" % (g, half), align_bytes=64)
-            nc.vector.quantize_mx(codes[:].bitcast(FP8X4), plane[:], signed[:].rearrange("p s t -> p (s t)"))
+            for first, last in pieces:
+                signs = sign[:, g : g + 1, :].to_broadcast([P, last - first, PACK])
+                nc.vector.tensor_tensor(signed[:, first:last], squares[g, half][:, first:last], signs, ALU.mult)
+                nc.vector.quantize_mx(codes[:, first:last].bitcast(FP8X4), plane[:, first:last], signed[:, first:last].rearrange("p s t -> p (s t)"))
             h_codes[g, half], h_planes[g, half] = codes, plane
 
         def down_bank(half, n):
@@ -208,75 +214,71 @@ def tile_list_paged_squared_relu_kernel(tc, tab, offs, w1, b1, gain, w2_words, w
         early = range(DOWN_BANKS)
         late = range(DOWN_BANKS, N_TILES)
         gather_scales(0)
-        gather_words(0)
         quantise_w1(0)
-        w2_codes, w2_planes, b2_sb = load_w2()
-        gather_scales(1)
-        quantise_w1(1)
+        gather_words(0)
         up(0, 0, 0)
         up(0, 0, 1)
         up(0, 0, 2)
         up(0, 0, 3)
-        gather_words(1)
-        quantise_w1(2)
-        square(0, 0, 416, 512, False)
-        up(1, 0, 0)
-        square(0, 0, 0, 208, True)
-        up(1, 0, 1)
-        up(1, 0, 2)
-        square(0, 0, 208, 416, True)
-        up(1, 0, 3)
+        square(0, 0, 0, 320, True)
+        square(0, 0, 320, 512, False)
         quantise_h(0, 0)
-        square(1, 0, 160, 512, False)
-        up(2, 0, 0)
-        square(1, 0, 0, 80, True)
-        up(2, 0, 1)
-        up(2, 0, 2)
-        square(1, 0, 80, 160, True)
-        up(2, 0, 3)
-        quantise_h(1, 0)
-        square(2, 0, 0, 224, True)
-        square(2, 0, 224, 512, False)
-        quantise_h(2, 0)
+        gather_scales(1)
+        gather_words(1)
+        quantise_w1(1)
+        quantise_w1(2)
         up(0, 1, 0)
         up(0, 1, 1)
         up(0, 1, 2)
         up(0, 1, 3)
+        square(0, 1, 320, 512, False)
+        up(1, 0, 0)
+        square(0, 1, 0, 80, True)
+        up(1, 0, 1)
+        square(0, 1, 80, 160, True)
+        up(1, 0, 2)
+        square(0, 1, 160, 240, True)
+        up(1, 0, 3)
+        square(0, 1, 240, 320, True)
+        quantise_h(0, 1)
+        square(1, 0, 0, 160, True)
+        square(1, 0, 160, 512, False)
+        quantise_h(1, 0)
+        up(2, 0, 0)
+        up(2, 0, 1)
+        up(2, 0, 2)
+        up(2, 0, 3)
+        square(2, 0, 0, 416, True)
+        square(2, 0, 416, 512, False)
+        quantise_h(2, 0)
+        up(1, 1, 0)
+        up(1, 1, 1)
+        up(1, 1, 2)
+        up(1, 1, 3)
+        square(1, 1, 0, 192, True)
+        square(1, 1, 192, 512, False)
+        quantise_h(1, 1)
+        up(2, 1, 0)
+        up(2, 1, 1)
+        up(2, 1, 2)
+        up(2, 1, 3)
         for g in range(2):
             for n in early:
                 down_pass(g, 0, n)
         for n in early:
             down_pass(2, 0, n)
             finish(0, n)
-        square(0, 1, 160, 512, False)
-        up(1, 1, 0)
-        square(0, 1, 0, 80, True)
-        up(1, 1, 1)
-        up(1, 1, 2)
-        square(0, 1, 80, 160, True)
-        up(1, 1, 3)
-        quantise_h(0, 1)
-        square(1, 1, 256, 512, False)
-        up(2, 1, 0)
-        square(1, 1, 0, 128, True)
-        up(2, 1, 1)
-        up(2, 1, 2)
-        square(1, 1, 128, 256, True)
-        up(2, 1, 3)
-        quantise_h(1, 1)
-        square(2, 1, 0, 448, True)
+        square(2, 1, 256, 448, True)
+        square(2, 1, 0, 256, True)
         square(2, 1, 448, 512, False)
-        quantise_h(2, 1)
+        quantise_h(2, 1, ((256, 512), (0, 256)))
         for n in late:
             for g in range(GROUPS):
                 down_pass(g, 0, n)
             finish(0, n)
         for n in early:
             down_pass(0, 1, n)
-        for n in late:
-            down_pass(0, 1, n)
-        for n in range(N_TILES):
-            down_pass(1, 1, n)
-        for n in range(N_TILES):
-            down_pass(2, 1, n)
+        for n in [4, 5, 6, 7, 0, 1, 2, 3]:
+            for g in range(1 if n in early else 0, GROUPS):
+                down_pass(g, 1, n)
             finish(1, n)

from contextlib import ExitStack

import concourse.mybir as mybir

K, T, S, H, N = 1024, 2048, 1024, 1536, 1024
FLOPS = 2 * K * H * S + 2 * H * N * S

F32 = mybir.dt.float32
BF16 = mybir.dt.bfloat16
I32 = mybir.dt.int32
U32 = mybir.dt.uint32
U16 = mybir.dt.uint16
U8 = mybir.dt.uint8
FP8X4 = mybir.dt.float8_e4m3fn_x4
FP4X4 = mybir.dt.float4_e2m1fn_x4
ACT = mybir.ActivationFunctionType
ALU = mybir.AluOpType

P = 128
PACK = 4
K_PASS = P * PACK
TOK = 512
UP_PASSES = K // K_PASS
GROUPS = H // K_PASS
HALVES = S // TOK
N_TILES = N // P
SQRT_FLOOR = 2.0**-100
UP_BANKS = 4
DOWN_BANKS = 4
PRE = 0
SCALAR_CASTS = [[128, 96], [96, 0], [0, 0]]
SCALAR_EVICTS = [[0, 4], [0, 6], [0, 7], [1, 1], [1, 3], [1, 5], [1, 7]]
SLOT = {(1, 1): 'w1_raw_0_0', 1: 'w1_raw_0_1'}


def tile_list_paged_squared_relu_kernel(tc, tab, offs, w1, b1, gain, w2_words, w2_scales, b2, out):
    nc = tc.nc
    with ExitStack() as ctx:
        keep = ctx.enter_context(tc.tile_pool(name="keep", bufs=1))
        ring = ctx.enter_context(tc.tile_pool(name="ring", bufs=3))
        psum = ctx.enter_context(tc.psum_pool(name="psum", bufs=1))

        gain_sb = keep.tile([P, GROUPS, PACK], F32, name="gain_sb")
        b1_sb = keep.tile([P, GROUPS, PACK], F32, name="b1_sb")
        nc.sync.dma_start(gain_sb[:], gain.rearrange("(g p t) -> p g t", p=P, t=PACK))
        nc.scalar.dma_start(b1_sb[:], b1.rearrange("(g p t) -> p g t", p=P, t=PACK))
        offsets = keep.tile([P, S // 16], U16, name="offsets")
        nc.sync.dma_start(offsets[:], offs)

        tab_scales = keep.tile([P, UP_PASSES, T // 4], I32, name="tab_scales", align_bytes=64)
        flat_scales = tab_scales[:].rearrange("p h t -> p (h t)")
        nc.vector.memset(flat_scales[:, :768], 0)
        nc.gpsimd.memset(flat_scales[:, 768:], 0)
        width = GROUPS * PACK
        gain_flat = gain_sb[:].rearrange("p g t -> p (g t)")
        sign = keep.tile([P, GROUPS, PACK], BF16, name="sign")
        flipped = keep.tile([P, width], F32, name="flipped")
        negative = keep.tile([P, width], F32, name="negative")
        clamped = keep.tile([P, width], F32, name="clamped")
        guess = keep.tile([P, width], F32, name="guess")
        inverse = keep.tile([P, width], F32, name="inverse")
        half_ratio = keep.tile([P, width], F32, name="half_ratio")
        root = keep.tile([P, width], F32, name="root")
        root_b1 = keep.tile([P, width], F32, name="root_b1")
        nc.vector.tensor_scalar(flipped[:], gain_flat, -1.0, SQRT_FLOOR, ALU.mult, ALU.max)
        nc.vector.tensor_scalar(negative[:], gain_flat, 0.0, None, ALU.is_lt)
        nc.vector.tensor_tensor(clamped[:], flipped[:], gain_flat, ALU.max)
        nc.vector.scalar_tensor_tensor(sign[:].rearrange("p g t -> p (g t)"), gain_flat, 0.0, negative[:], ALU.is_gt, ALU.subtract)
        nc.scalar.activation(guess[:], clamped[:], ACT.Sqrt)
        nc.vector.reciprocal(inverse[:], guess[:])
        nc.vector.scalar_tensor_tensor(half_ratio[:], clamped[:], 0.5, inverse[:], ALU.mult, ALU.mult)
        nc.vector.scalar_tensor_tensor(root[:], guess[:], 0.5, half_ratio[:], ALU.mult, ALU.add)
        nc.vector.tensor_tensor(root_b1[:], root[:], b1_sb[:].rearrange("p g t -> p (g t)"), ALU.mult)

        scale_rows = tab[0, 512 * T :].rearrange("(h q r t) -> q r h t", h=UP_PASSES, q=4, r=4).bitcast(I32)
        for q in range(4):
            nc.sync.dma_start(tab_scales[32 * q : 32 * q + 4], scale_rows[q])
        w1_raw = {}

        def load_w1(g, a):
            raw = keep.tile([P, PACK, K_PASS], F32, name="w1_raw_%d_%d" % (g, a), align_bytes=64)
            rows = w1[a * K_PASS : (a + 1) * K_PASS, g * K_PASS : (g + 1) * K_PASS]
            nc.sync.dma_start(raw[:], rows.rearrange("(p j) c -> p j c", j=PACK))
            w1_raw[g, a] = raw

        def load_w2():
            planes = keep.tile([P, GROUPS, N // 4], I32, name="w2_planes", align_bytes=64)
            nc.gpsimd.memset(planes[:], 0)
            rows = w2_scales.rearrange("a (q r) n -> q r a n", r=4).bitcast(I32)
            for q in range(4):
                nc.sync.dma_start(planes[32 * q : 32 * q + 4], rows[q])
            codes = keep.tile([P, GROUPS, N // 2], I32, name="w2_codes", align_bytes=64)
            nc.sync.dma_start(codes[:], w2_words.rearrange("a p n -> p a n").bitcast(I32))
            bias = keep.tile([P, N_TILES], F32, name="b2_sb", align_bytes=64)
            with nc.allow_non_contiguous_dma("one bias value for each partition"):
                nc.sync.dma_start(bias[:], b2.rearrange("(j p) -> p j", p=P))
            return codes, planes, bias

        pieces = [(g, a) for g in range(GROUPS) for a in range(UP_PASSES)]
        for g, a in pieces[:PRE]:
            load_w1(g, a)
        tab_words = keep.tile([P, T], I32, name="tab_words", align_bytes=64)
        nc.sync.dma_start(tab_words[:], tab[0, : 512 * T].rearrange("(p t) -> p t", p=P).bitcast(I32))
        for g, a in pieces[PRE:6]:
            load_w1(g, a)

        w2_codes, w2_planes, b2_sb = load_w2()
        for g, a in pieces[6:]:
            load_w1(g, a)

        v_codes, v_planes = {}, {}

        def gather_scales(half):
            window_offsets = offsets[:, half * (TOK // 16) : (half + 1) * (TOK // 16)]
            for a in range(UP_PASSES):
                plane = keep.tile([P, TOK], U8, name="v_plane_%d_%d" % (half, a), tag=SLOT.get((half, a), "v_plane_%d_%d" % (half, a)), align_bytes=64)
                nc.vector.tensor_copy(plane[:], tab_scales[:, a, :].bitcast(U8).indirect(window_offsets))
                v_planes[half, a] = plane

        def gather_words(half):
            window_offsets = offsets[:, half * (TOK // 16) : (half + 1) * (TOK // 16)]
            pairs = keep.tile([P, TOK], U32, name="v_pairs_%d" % half, tag=SLOT.get(half, "v_pairs_%d" % half), align_bytes=64)
            nc.vector.tensor_copy(pairs[:], tab_words[:].bitcast(U32).indirect(window_offsets))
            parted = keep.tile([P, UP_PASSES, 2 * TOK], U8, name="v_codes_%d" % half, align_bytes=64)
            nc.vector.tensor_copy(parted[:].bitcast(U16), pairs[:].bitcast(U16).rearrange("p (j h) -> p h j", h=2))
            v_codes[half] = parted

        w1_codes, w1_planes = {}, {}

        def quantise_w1(g, passes=range(UP_PASSES)):
            for a in passes:
                raw = w1_raw[g, a]
                grouped = keep.tile([P, PACK * K_PASS], BF16, name="w1_grouped_%d_%d" % (g, a), align_bytes=64)
                dst = grouped[:].rearrange("p (t m j) -> p m j t", t=PACK, j=PACK)
                src = raw[:].rearrange("p j (m t) -> p m j t", t=PACK)
                split = SCALAR_CASTS[g][a]
                if split > 0:
                    nc.scalar.copy(dst[:, :split], src[:, :split])
                if split < P:
                    nc.vector.tensor_copy(dst[:, split:], src[:, split:])
                codes = keep.tile([P, K_PASS], U32, name="w1_codes_%d_%d" % (g, a), align_bytes=64)
                plane = keep.tile([P, K_PASS], U8, name="w1_plane_%d_%d" % (g, a), align_bytes=64)
                nc.vector.quantize_mx(codes[:].bitcast(FP8X4), plane[:], grouped[:])
                w1_codes[g, a], w1_planes[g, a] = codes, plane

        banks = [psum.tile([P, TOK], F32, name="bank_%d" % b) for b in range(UP_BANKS + DOWN_BANKS)]
        h_codes, h_planes = {}, {}

        relus, squares = {}, {}

        def up(g, half, t):
            if t == 0:
                relus[g, half] = ring.tile([P, PACK, TOK], F32, name="relu")
            unit = len(relus) - 1
            bank = banks[(unit * PACK + t) % UP_BANKS]
            cols = slice(t * P, (t + 1) * P)
            for a in range(UP_PASSES):
                nc.tensor.matmul_mx(
                    out=bank[:],
                    lhsT=w1_codes[g, a][:, cols].bitcast(FP8X4),
                    lhsT_scale=w1_planes[g, a][:, cols],
                    rhs=v_codes[half][:, a, :].bitcast(FP4X4),
                    rhs_scale=v_planes[half, a][:],
                    start=(a == 0),
                    stop=(a == UP_PASSES - 1),
                )
            c = g * PACK + t
            nc.scalar.activation(relus[g, half][:, t, :], bank[:], ACT.Relu, bias=root_b1[:, c : c + 1], scale=root[:, c : c + 1])

        def square(g, half, first, last, on_scalar):
            if (g, half) not in squares:
                squares[g, half] = ring.tile([P, TOK, PACK], BF16, name="squared", align_bytes=64)
            src = relus[g, half][:].rearrange("p t (c i) -> p c t i", i=4)[:, first // 4 : last // 4]
            dst = squares[g, half][:].rearrange("p (c i) t -> p c t i", i=4)[:, first // 4 : last // 4]
            if on_scalar:
                nc.scalar.activation(dst, src, ACT.Square)
            else:
                nc.vector.tensor_tensor(dst, src, src, ALU.mult)

        def quantise_h(g, half, pieces=((0, TOK),)):
            signed = ring.tile([P, TOK, PACK], BF16, name="signed", align_bytes=64)
            codes = keep.tile([P, TOK], U32, name="h_codes_%d_%d" % (g, half), align_bytes=64)
            plane = keep.tile([P, TOK], U8, name="h_plane_%d_%d" % (g, half), align_bytes=64)
            for first, last in pieces:
                signs = sign[:, g : g + 1, :].to_broadcast([P, last - first, PACK])
                nc.vector.tensor_tensor(signed[:, first:last], squares[g, half][:, first:last], signs, ALU.mult)
                nc.vector.quantize_mx(codes[:, first:last].bitcast(FP8X4), plane[:, first:last], signed[:, first:last].rearrange("p s t -> p (s t)"))
            h_codes[g, half], h_planes[g, half] = codes, plane

        def down_bank(half, n):
            if half == HALVES - 1 and n >= DOWN_BANKS:
                return banks[n - DOWN_BANKS]
            return banks[UP_BANKS + (half * N_TILES + n) % DOWN_BANKS]

        def down_pass(g, half, n):
            nc.tensor.matmul_mx(
                out=down_bank(half, n)[:],
                lhsT=w2_codes[:, g, :].bitcast(U8)[:, 2 * n * P : 2 * (n + 1) * P].bitcast(FP4X4),
                lhsT_scale=w2_planes[:, g, :].bitcast(U8)[:, n * P : (n + 1) * P],
                rhs=h_codes[g, half][:].bitcast(FP8X4),
                rhs_scale=h_planes[g, half][:],
                start=(g == 0),
                stop=(g == GROUPS - 1),
            )

        def finish(half, n):
            result = keep.tile([P, TOK], F32, name="result_%d_%d" % (half, n))
            if [half, n] in SCALAR_EVICTS:
                nc.scalar.activation(result[:], down_bank(half, n)[:], ACT.Identity, bias=b2_sb[:, n : n + 1])
            else:
                nc.vector.tensor_scalar(result[:], down_bank(half, n)[:], b2_sb[:, n : n + 1], None, ALU.add)
            nc.sync.dma_start(out[n * P : (n + 1) * P, half * TOK : (half + 1) * TOK], result[:])

        early = range(DOWN_BANKS)
        late = range(DOWN_BANKS, N_TILES)
        gather_scales(0)
        quantise_w1(0)
        gather_words(0)
        up(0, 0, 0)
        up(0, 0, 1)
        up(0, 0, 2)
        up(0, 0, 3)
        square(0, 0, 0, 320, True)
        square(0, 0, 320, 512, False)
        quantise_h(0, 0)
        gather_scales(1)
        gather_words(1)
        quantise_w1(1)
        quantise_w1(2)
        up(0, 1, 0)
        up(0, 1, 1)
        up(0, 1, 2)
        up(0, 1, 3)
        square(0, 1, 320, 512, False)
        up(1, 0, 0)
        square(0, 1, 0, 80, True)
        up(1, 0, 1)
        square(0, 1, 80, 160, True)
        up(1, 0, 2)
        square(0, 1, 160, 240, True)
        up(1, 0, 3)
        square(0, 1, 240, 320, True)
        quantise_h(0, 1)
        square(1, 0, 0, 160, True)
        square(1, 0, 160, 512, False)
        quantise_h(1, 0)
        up(2, 0, 0)
        up(2, 0, 1)
        up(2, 0, 2)
        up(2, 0, 3)
        square(2, 0, 0, 416, True)
        square(2, 0, 416, 512, False)
        quantise_h(2, 0)
        up(1, 1, 0)
        up(1, 1, 1)
        up(1, 1, 2)
        up(1, 1, 3)
        square(1, 1, 0, 192, True)
        square(1, 1, 192, 512, False)
        quantise_h(1, 1)
        up(2, 1, 0)
        up(2, 1, 1)
        up(2, 1, 2)
        up(2, 1, 3)
        for g in range(2):
            for n in early:
                down_pass(g, 0, n)
        for n in early:
            down_pass(2, 0, n)
            finish(0, n)
        square(2, 1, 256, 448, True)
        square(2, 1, 0, 256, True)
        square(2, 1, 448, 512, False)
        quantise_h(2, 1, ((256, 512), (0, 256)))
        for n in late:
            for g in range(GROUPS):
                down_pass(g, 0, n)
            finish(0, n)
        for n in early:
            down_pass(0, 1, n)
        for n in [4, 5, 6, 7, 0, 1, 2, 3]:
            for g in range(1 if n in early else 0, GROUPS):
                down_pass(g, 1, n)
            finish(1, n)
